import numpy as np, ml_dtypes
CORES = [17,57,65,89,97,121]
N = 6
W, KW, DIL = 512, 5, 1
H = (KW // 2) * DIL
def setup_inputs(rng):
    return {"x": rng.standard_normal((N, 128, W), dtype=np.float32).astype(ml_dtypes.bfloat16), "w": rng.standard_normal((N, 128, KW * 128), dtype=np.float32).astype(ml_dtypes.bfloat16)}
def setup_inputs_big(rng):
    d = setup_inputs(rng)
    for k in ("x", "w"): d[k] = (d[k].astype(np.float32) * 1024.0).astype(d[k].dtype)
    return d
def setup_inputs_small(rng):
    d = setup_inputs(rng)
    for k in ("x", "w"): d[k] = (d[k].astype(np.float32) * (1 / 1024.0)).astype(d[k].dtype)
    return d
def reference(x, w):
    X, W_ = x.astype(np.float64), w.astype(np.float64)
    g = np.concatenate(list(X), axis=1)
    p = np.concatenate([g[:, -H:], g, g[:, :H]], axis=1)
    y = np.zeros((N, 128, W))
    for r in range(N):
        for i in range(KW):
            y[r] += W_[r][:, 128 * i:128 * i + 128].T @ p[:, W * r + i * DIL:W * r + i * DIL + W]
    return {"y": y.astype(ml_dtypes.bfloat16 if x.dtype != np.float64 else np.float64)}

from concourse.bass import DstId, RemoteDMATransfer

P, W, KW, H = 128, 512, 5, 2
HALF = (W - 2 * H) // 2
FWD_ENGINES = 4

SCRATCH = {
    "stage": ("dram", [2, P, H], "bfloat16"),
    "halo": ("sbuf", [P, 2 * H], "bfloat16"),
    "xs": ("sbuf", [P, W], "bfloat16"),
    "ws": ("sbuf", [P, KW * P], "bfloat16"),
    "ys": ("sbuf", [P, W], "bfloat16"),
    "yb": ("sbuf", [P, 16], "bfloat16"),
    "pa": ("psum", [P, 512], "float32"),
    "pb": ("psum", [P, 512], "float32"),
    "pl": ("psum", [P, 512], "float32"),
    "pr": ("psum", [P, 512], "float32"),
}
SEMAPHORES = ["edge", "ld", "sent", "got", "hl", "hr", "ma", "mb", "ml", "mr", "ca", "cb", "cl", "cr", "st"]


def _engines(mask, count, skip=0):
    bits = [b for b in range(mask.bit_length()) if (mask >> b) & 1]
    m = 0
    for b in bits[skip:skip + count]:
        m |= 1 << b
    return m


def _plan(T, topo):
    cores = list(T.cores)
    n = len(cores)
    every = range(topo.CHIPS * topo.CORES_PER_CHIP)
    plan, used = {}, set(cores)
    for r, c in enumerate(cores):
        for slot, d in ((0, cores[(r - 1) % n]), (1, cores[(r + 1) % n])):
            cand = [h for h in every if topo.chip(h) == topo.chip(c) and h not in used
                    and topo.may_write(c, h) and topo.may_write(h, d)]
            cand.sort(key=lambda h: (topo.die(h) != topo.die(c), h))
            plan[(c, slot)] = (cand[0], d)
            used.add(cand[0])
    return plan


def _border_terms():
    lo, lh, ro, rh = [], [], [], []
    for i in range(KW):
        nh = max(0, H - i)
        if nh < H:
            lo.append((i, nh, H, nh + i - H))
        if nh > 0:
            lh.append((i, 0, nh, i))
        no = max(0, min(H, 2 * H - i))
        if no > 0:
            ro.append((i, 0, no, W - 2 * H + i))
        if no < H:
            rh.append((i, no, H, no + i - 2 * H))
    lo.sort(key=lambda t: t[1])
    ro.sort(key=lambda t: -t[2])
    return lo, lh, ro, rh


def _helper(g, core, T, topo, slot, dst):
    rid, pid, _ = topo.addr(dst)
    out = T.halo[:, H:2 * H] if slot == 0 else T.halo[:, 0:H]
    sem = T.sem.hr if slot == 0 else T.sem.hl
    g.wait_ge(T.sem.got, 1)
    g.remote_dma(out_ap=out, in_ap=T.stage[slot], remote_sem=sem, local_sem=T.sem.sent, pid=pid, routing_id=rid,
                 dma_engine_mask=_engines(topo.mask(core, dst), FWD_ENGINES))
    g.wait_ge(T.sem.sent, FWD_ENGINES)


def rank_program(g, core, T, topo):
    plan = _plan(T, topo)
    rank = T.rank_of(core)
    if rank is None:
        for (src, slot), (h, dst) in plan.items():
            if h == core:
                _helper(g, core, T, topo, slot, dst)
        return

    s = T.sem
    g.sync.dma_start(T.stage[0], T.x[:, 0:H]).then_inc(s.edge, 16)
    g.scalar.dma_start(T.stage[1], T.x[:, W - H:W]).then_inc(s.edge, 16)
    g.sync.dma_start(T.ws[:, :], T.w[:, :]).then_inc(s.ld, 16)
    g.scalar.dma_start(T.xs[:, :], T.x[:, :]).then_inc(s.ld, 16)

    g.wait_ge(s.edge, 32)
    transfers = []
    for slot in (0, 1):
        h = plan[(core, slot)][0]
        rid, pid, _ = topo.addr(h)
        transfers.append(RemoteDMATransfer(dst_ids=[DstId(rid=rid, pnc=pid)],
                                           dma_engine_mask=_engines(topo.mask(core, h), 1, skip=slot),
                                           remote_sem=s.got, src=T.stage[slot], dst=T.stage[slot]))
    g.remote_dma_fused(transfers, local_sem=s.sent)

    def tap(i):
        return T.ws[:, P * i:P * i + P]

    g.tensor.wait_ge(s.ld, 32)
    for half, (bank, done) in enumerate(((T.pa, s.ma), (T.pb, s.mb))):
        for i in range(KW):
            mm = g.tensor.matmul(bank[:, 0:HALF], tap(i), T.xs[:, half * HALF + i:half * HALF + i + HALF],
                                 i == 0, i == KW - 1)
        mm.then_inc(done, 1)
    lo, lh, ro, rh = _border_terms()
    for bank, own in ((T.pl, lo), (T.pr, ro)):
        for k, (i, a, b, c0) in enumerate(own):
            g.tensor.matmul(bank[:, a:b], tap(i), T.xs[:, c0:c0 + b - a], k == 0, False)
    for bank, terms, base, landed, done in ((T.pl, lh, 0, s.hl, s.ml), (T.pr, rh, H, s.hr, s.mr)):
        g.tensor.wait_ge(landed, FWD_ENGINES)
        for k, (i, a, b, c0) in enumerate(terms):
            mm = g.tensor.matmul(bank[:, a:b], tap(i), T.halo[:, base + c0:base + c0 + b - a],
                                 False, k == len(terms) - 1)
        mm.then_inc(done, 1)

    g.vector.wait_ge(s.ma, 1)
    g.vector.tensor_copy(T.ys[:, H:H + HALF], T.pa[:, 0:HALF]).then_inc(s.ca, 1)
    g.vector.wait_ge(s.mb, 1)
    g.vector.tensor_copy(T.ys[:, H + HALF:W - H], T.pb[:, 0:HALF]).then_inc(s.cb, 1)
    g.vector.wait_ge(s.ml, 1)
    g.vector.tensor_copy(T.yb[:, 0:H], T.pl[:, 0:H]).then_inc(s.cl, 1)
    g.vector.wait_ge(s.mr, 1)
    g.vector.tensor_copy(T.yb[:, 8:8 + H], T.pr[:, 0:H]).then_inc(s.cr, 1)

    g.sync.wait_ge(s.ca, 1)
    g.sync.dma_start(T.y[:, H:H + HALF], T.ys[:, H:H + HALF]).then_inc(s.st, 16)
    g.scalar.wait_ge(s.cb, 1)
    g.scalar.dma_start(T.y[:, H + HALF:W - H], T.ys[:, H + HALF:W - H]).then_inc(s.st, 16)
    g.sync.wait_ge(s.cl, 1)
    g.sync.dma_start(T.y[:, 0:H], T.yb[:, 0:H]).then_inc(s.st, 16)
    g.scalar.wait_ge(s.cr, 1)
    g.scalar.dma_start(T.y[:, W - H:W], T.yb[:, 8:8 + H]).then_inc(s.st, 16)

    g.wait_ge(s.sent, 2)
    g.wait_ge(s.st, 64)
